import numpy as np
import ml_dtypes


def mxq(x, axis, fmt="e4m3"):
    dtype, down = {"e4m3": (ml_dtypes.float8_e4m3fn, 7), "e5m2": (ml_dtypes.float8_e5m2, 14)}[fmt]
    v = np.moveaxis(np.asarray(x, np.float32).astype(ml_dtypes.bfloat16).astype(np.float64), axis, -1)
    blocks = v.reshape(v.shape[:-1] + (-1, 32))
    amax = np.abs(blocks).max(-1, keepdims=True)
    byte = np.maximum(np.where(amax > 0, np.frexp(amax)[1] - 1 + 127, 0) - down, 1)
    scale = np.exp2(byte - 127.0)
    codes = (blocks / scale).astype(np.float32).astype(dtype).astype(np.float64)
    return np.moveaxis((codes * scale).reshape(v.shape), -1, axis)


WIDE = False


def mx_kscale(k):
    if not WIDE:
        return np.ones(k)
    levels = np.array([10, -10, 5, -5, 0])
    if k % 512:
        return np.exp2(np.random.permutation(np.resize(levels, k // 32))).repeat(32)
    a = np.empty((k // 512, 16))
    for p in range(k // 512):
        a[p, :8] = np.random.permutation(np.resize(levels, 8))
        for g in range(8):
            far = levels[np.abs(levels - a[p, g]) >= 10]
            a[p, g + 8] = far[np.random.randint(len(far))]
    return np.exp2(a.ravel()).repeat(32)


def f64(x):
    return np.asarray(x).astype(np.float64)


def striped(idx):
    return np.tile(np.asarray(idx).reshape(-1, 16).T, (8, 1)).astype(np.uint16)


def unstriped(offs):
    return offs[:16].T.reshape(-1).astype(np.int64)


def bf(x):
    return np.asarray(x, np.float32).astype(ml_dtypes.bfloat16)


def planes(Y):
    r, m = Y.shape
    b = f64(bf(Y)).reshape(r // 32, 32, m)
    amax = np.abs(b).max(1)
    byte = np.clip(np.where(amax > 0, np.frexp(amax)[1] - 1 + 127 - 7, 1), 1, 254)
    codes = (b * np.exp2(127.0 - byte)[:, None, :]).reshape(r, m).astype(np.float32).astype(ml_dtypes.float8_e4m3fn).view(np.uint8)
    words = codes.reshape(r // 512, 128, 4, m).transpose(0, 1, 3, 2)
    return np.ascontiguousarray(words), np.ascontiguousarray(byte.astype(np.uint8).reshape(r // 512, 16, m))


D, T, I, Q = 512, 1024, 256, 512


def setup_inputs():
    n = np.random.standard_normal
    idx = np.random.permutation(T)[:I]
    idx2 = np.random.permutation(T)[:I]
    fd = mx_kscale(D)
    fq = mx_kscale(Q)
    return {
        "query": (n((D, Q)) * 0.6 / np.sqrt(D) * fd[:, None]).astype(np.float32),
        "keys": (n((D, T)) / fd[:, None]).astype(np.float32),
        "mass": np.tile(np.random.uniform(0.5, 4.0, T), (128, 1)).astype(np.float32),
        "target": (np.random.uniform(0.0, 0.008, (Q, I))).astype(np.float32),
        "qs": (np.random.uniform(16.0, 64.0, (Q, 1)) * fq[:, None]).astype(np.float32),
        "qrows": (n((Q, D)) / fq[:, None]).astype(np.float32),
        "old": (n((D, T)) * 1.0).astype(np.float32),
        "offs": striped(idx),
        "offs2": striped(idx2),
    }


def reference(query, keys, mass, target, qs, qrows, old, offs, offs2):
    idx = unstriped(offs)
    idx2 = unstriped(offs2)
    km = (f64(keys)[:, idx] * f64(mass)[:1][:, idx] + f64(keys)[:, idx2] * f64(mass)[:1][:, idx2]) / (f64(mass)[:1][:, idx] + f64(mass)[:1][:, idx2])
    queryq = mxq(f64(query), 0, "e4m3")
    kmq = mxq(km, 0, "e4m3")
    a = queryq.T @ kmq
    s = a + np.log(f64(mass)[:1][:, idx] + f64(mass)[:1][:, idx2])
    p = np.exp(s - np.max(s, axis=1, keepdims=True))
    ds = (p / np.sum(p, axis=1, keepdims=True) - f64(target)) * f64(qs)
    qrowsq = mxq(f64(qrows), 0, "e4m3")
    dsq = mxq(ds, 0, "e4m3")
    gk = qrowsq.T @ dsq
    g1 = gk * f64(mass)[:1][:, idx] / (f64(mass)[:1][:, idx] + f64(mass)[:1][:, idx2])
    g2 = gk * f64(mass)[:1][:, idx2] / (f64(mass)[:1][:, idx] + f64(mass)[:1][:, idx2])
    fa = np.zeros((D, T))
    fa[:, idx] = g1
    fb = np.zeros((D, T))
    fb[:, idx2] = g2
    y = f64(old) + fa + fb
    words, scales = planes(y)
    return y, words, scales

@@ -1,0 +1,227 @@
+from contextlib import ExitStack
+
+import concourse.mybir as mybir
+
+D, T, I, Q = 512, 1024, 256, 512
+FLOPS = 2 * D * Q * I * 2
+
+F32 = mybir.dt.float32
+BF16 = mybir.dt.bfloat16
+I32 = mybir.dt.int32
+U32 = mybir.dt.uint32
+U16 = mybir.dt.uint16
+U8 = mybir.dt.uint8
+FP8X4 = mybir.dt.float8_e4m3fn_x4
+ALU = mybir.AluOpType
+ACT = mybir.ActivationFunctionType
+AX = mybir.AxisListType
+
+P = 128
+PACK = 4
+RUN = 4
+CHUNKS = 4
+CW = T // CHUNKS
+
+
+def tile_attend_bmassmerge_pl_kernel(tc, query, keys, mass, target, qs, qrows, old, offs, offs2, out_0, out_1, out_2):
+    nc = tc.nc
+    with ExitStack() as ctx:
+        lists = ctx.enter_context(tc.tile_pool(name="lists", bufs=1))
+        sb = ctx.enter_context(tc.tile_pool(name="sb", bufs=1))
+        ps = ctx.enter_context(tc.psum_pool(name="ps", bufs=1))
+
+        list_t = [lists.tile([P, I // 16], U16, name="list%d" % n) for n in range(2)]
+        nc.sync.dma_start(list_t[0][:], offs)
+        nc.sync.dma_start(list_t[1][:], offs2)
+
+        mass_t = sb.tile([P, T], F32, name="mass_t")
+        nc.sync.dma_start(mass_t[:], mass)
+        keys_v = keys.rearrange("(p j) t -> p j t", j=PACK)
+        key_t = [sb.tile([P, T], F32, name="key%d" % j) for j in range(PACK)]
+        for j in range(PACK):
+            nc.sync.dma_start(key_t[j][:], keys_v[:, j, :])
+
+        def load_halves(src, name):
+            view = src.rearrange("(p j) c -> p j c", j=PACK)
+            halves = [sb.tile([P, PACK, 256], F32, name="%s%d" % (name, h)) for h in range(2)]
+            for h in range(2):
+                nc.sync.dma_start(halves[h][:], view[:, :, 256 * h : 256 * (h + 1)])
+            return halves
+
+        query_h = load_halves(query, "query_raw")
+        qrows_h = load_halves(qrows, "qrows_raw")
+        qs_t = sb.tile([P, PACK], F32, name="qs_t")
+        nc.sync.dma_start(qs_t[:], qs.rearrange("(s r) o -> s (r o)", r=PACK))
+        target_t = sb.tile([P, PACK, I], F32, name="target_t")
+        nc.sync.dma_start(target_t[:], target.rearrange("(s r) i -> s r i", r=PACK))
+        old_v = old.rearrange("(p j) t -> p j t", j=PACK)
+        old_t = [sb.tile([P, T], F32, name="old%d" % j) for j in range(PACK)]
+        for j in range(PACK):
+            nc.sync.dma_start(old_t[j][:], old_v[:, j, :])
+
+        win = [[sb.tile([P, T], F32, name="win%d_%d" % (n, b)) for b in range(2)] for n in range(2)]
+        for b in range(2):
+            for n in range(2):
+                nc.vector.memset(win[n][b][:], 0.0)
+
+        m12 = sb.tile([P, 2, I], F32, name="m12")
+        for n in range(2):
+            nc.vector.tensor_copy(m12[:, n, :], mass_t[:].indirect(list_t[n][:]))
+        msum = sb.tile([P, I], F32, name="msum")
+        nc.vector.tensor_tensor(msum[:], m12[:, 0, :], m12[:, 1, :], ALU.add)
+        lnm = sb.tile([P, I], F32, name="lnm")
+        nc.scalar.activation(lnm[:], msum[:], ACT.Ln)
+        seed = sb.tile([P, I], F32, name="seed")
+        nc.scalar.activation(seed[:], lnm[:], ACT.Exp, scale=-1.0)
+
+        def deal(halves, name):
+            dealt = sb.tile([P, PACK, P, PACK], BF16, name=name + "_bf", align_bytes=64)
+            for h in range(2):
+                nc.scalar.copy(
+                    dealt[:, :, 64 * h : 64 * (h + 1), :].rearrange("p r s j -> p s j r"),
+                    halves[h][:].rearrange("p j (s r) -> p s j r", r=PACK),
+                )
+            return dealt
+
+        def quantise(src_flat, width, name):
+            codes = sb.tile([P, width], U32, name=name + "_codes", align_bytes=64)
+            scales = sb.tile([P, width], U8, name=name + "_scales", align_bytes=64)
+            nc.vector.quantize_mx(out=codes[:].bitcast(FP8X4), scales=scales[:], in_=src_flat)
+            return codes, scales
+
+        query_bf = deal(query_h, "query")
+        qrows_bf = deal(qrows_h, "qrows")
+        tq = sb.tile([P, PACK, I], F32, name="tq")
+        for r in range(PACK):
+            nc.scalar.activation(tq[:, r, :], target_t[:, r, :], ACT.Copy, scale=qs_t[:, r : r + 1])
+
+        wk = [sb.tile([P, PACK, I], F32, name="wk%d" % n) for n in range(2)]
+        resid = sb.tile([P, I], F32, name="resid")
+        rinv = sb.tile([P, I], F32, name="rinv")
+        for j in range(PACK):
+            for n in range(2):
+                nc.vector.tensor_tensor(wk[n][:, j, :], key_t[j][:].indirect(list_t[n][:]), m12[:, n, :], ALU.mult)
+            if j == 2:
+                nc.vector.scalar_tensor_tensor(resid[:], msum[:], -1.0, seed[:], ALU.mult, ALU.mult)
+        nc.vector.scalar_tensor_tensor(rinv[:], resid[:], 2.0, seed[:], ALU.add, ALU.mult)
+        ksum = sb.tile([P, PACK, I], F32, name="ksum")
+        nc.vector.tensor_tensor(ksum[:], wk[0][:], wk[1][:], ALU.add)
+        q_codes, q_scales = quantise(query_bf[:].rearrange("p r s j -> p (r s j)"), Q, "query")
+        km_bf = sb.tile([P, I, PACK], BF16, name="km_bf", align_bytes=64)
+        nc.vector.tensor_tensor(
+            km_bf[:].rearrange("p (c i) j -> p c j i", i=RUN),
+            ksum[:].rearrange("p j (c i) -> p c j i", i=RUN),
+            rinv[:].rearrange("p (c i) -> p c i", i=RUN).unsqueeze(2).to_broadcast([P, I // RUN, PACK, RUN]),
+            ALU.mult,
+        )
+        share = sb.tile([P, 2, I], F32, name="share")
+        nc.vector.tensor_tensor(share[:], m12[:], rinv[:].unsqueeze(1).to_broadcast([P, 2, I]), ALU.mult)
+        km_codes, km_scales = quantise(km_bf[:].rearrange("p i j -> p (i j)"), I, "km")
+
+        score = [ps.tile([P, 2, I], F32, name="score%d" % h) for h in range(2)]
+        for r in range(PACK):
+            cols = slice(P * r, P * (r + 1))
+            nc.tensor.matmul_mx(
+                out=score[r // 2][:, r % 2, :],
+                lhsT=q_codes[:, cols].bitcast(FP8X4), lhsT_scale=q_scales[:, cols],
+                rhs=km_codes[:].bitcast(FP8X4), rhs_scale=km_scales[:],
+                start=True, stop=True,
+            )
+        r_codes, r_scales = quantise(qrows_bf[:].rearrange("p r s j -> p (r s j)"), D, "qrows")
+
+        s_t = [sb.tile([P, 2, I], F32, name="s%d" % h) for h in range(2)]
+        negmax = [sb.tile([P, 2], F32, name="negmax%d" % h) for h in range(2)]
+        rowsum = [sb.tile([P, 2], F32, name="rowsum%d" % h) for h in range(2)]
+        rowinv = [sb.tile([P, 2], F32, name="rowinv%d" % h) for h in range(2)]
+        p_t = [sb.tile([P, 2, I], F32, name="p%d" % h) for h in range(2)]
+        pn = sb.tile([P, PACK, I], F32, name="pn")
+        for h in range(2):
+            nc.vector.tensor_tensor(s_t[h][:], score[h][:], lnm[:].unsqueeze(1).to_broadcast([P, 2, I]), ALU.add)
+        for h in range(2):
+            nc.vector.tensor_reduce(negmax[h][:], s_t[h][:], AX.X, ALU.max, negate=True)
+            for e in range(2):
+                nc.scalar.activation(p_t[h][:, e, :], s_t[h][:, e, :], ACT.Exp,
+                                     bias=negmax[h][:, e : e + 1], accum_out=rowsum[h][:, e : e + 1])
+        for h in range(2):
+            nc.vector.reciprocal(rowinv[h][:], rowsum[h][:])
+            for e in range(2):
+                r = 2 * h + e
+                nc.vector.tensor_scalar(pn[:, r, :], p_t[h][:, e, :], rowinv[h][:, e : e + 1], qs_t[:, r : r + 1],
+                                        ALU.mult, ALU.mult)
+        ds_bf = sb.tile([P, I, PACK], BF16, name="ds_bf", align_bytes=64)
+        nc.vector.tensor_tensor(
+            ds_bf[:].rearrange("p (c i) r -> p c r i", i=RUN),
+            pn[:].rearrange("p r (c i) -> p c r i", i=RUN),
+            tq[:].rearrange("p r (c i) -> p c r i", i=RUN),
+            ALU.subtract,
+        )
+        ds_codes, ds_scales = quantise(ds_bf[:].rearrange("p i r -> p (i r)"), I, "ds")
+
+        gk = []
+        for j in range(PACK):
+            cols = slice(P * j, P * (j + 1))
+            acc = ps.tile([P, I], F32, name="gk_acc%d" % j)
+            nc.tensor.matmul_mx(
+                out=acc[:],
+                lhsT=r_codes[:, cols].bitcast(FP8X4), lhsT_scale=r_scales[:, cols],
+                rhs=ds_codes[:].bitcast(FP8X4), rhs_scale=ds_scales[:],
+                start=True, stop=True,
+            )
+            gk.append(sb.tile([P, I], F32, name="gk%d" % j))
+            nc.scalar.copy(gk[j][:], acc[:])
+
+        out_v = out_0.rearrange("(p j) t -> p j t", j=PACK)
+        y = [sb.tile([P, 2, T], F32, name="y%d" % u) for u in range(2)]
+        y_bf = [sb.tile([P, CW, PACK], BF16, name="y_bf%d" % c, align_bytes=64) for c in range(CHUNKS)]
+
+        def scatter(n, j):
+            nc.vector.tensor_tensor(win[n][j % 2][:].indirect(list_t[n][:]), gk[j][:], share[:, n, :], ALU.mult)
+
+        def add_first(j):
+            nc.vector.tensor_tensor(y[j // 2][:, j % 2, :], old_t[j][:], win[0][j % 2][:], ALU.add)
+
+        def add_second(j, cols):
+            dst = y[j // 2][:, j % 2, cols]
+            nc.vector.tensor_tensor(dst, dst, win[1][j % 2][:, cols], ALU.add)
+
+        def weave(u, c, on_scalar):
+            dst = y_bf[c][:, :, 2 * u : 2 * u + 2].rearrange("p (c i) j -> p c j i", i=RUN)
+            src = y[u][:, :, CW * c : CW * (c + 1)].rearrange("p j (c i) -> p c j i", i=RUN)
+            if on_scalar:
+                nc.scalar.copy(dst, src)
+            else:
+                nc.vector.tensor_copy(dst, src)
+
+        whole = slice(0, T)
+        for j in range(PACK):
+            scatter(0, j)
+            if j > 0:
+                add_second(j - 1, whole)
+                nc.sync.dma_start(out_v[:, j - 1, :], y[(j - 1) // 2][:, (j - 1) % 2, :])
+            if j == 2:
+                for c in range(CHUNKS):
+                    weave(0, c, True)
+            scatter(1, j)
+            add_first(j)
+
+        y_codes = sb.tile([P, T], U32, name="y_codes", align_bytes=64)
+        y_scales = sb.tile([P, T], U8, name="y_scales", align_bytes=64)
+        words_v = out_1[0].rearrange("l c r -> l (c r)").bitcast(I32)
+        for c in range(CHUNKS):
+            add_second(PACK - 1, slice(CW * c, CW * (c + 1)))
+            if c < 2:
+                weave(1, c, True)
+            if c % 2 == 1:
+                half = slice(CW * (c - 1), CW * (c + 1))
+                nc.sync.dma_start(out_v[:, PACK - 1, half], y[1][:, 1, half])
+        for c in (2, 3):
+            weave(1, c, False)
+        for c in (0, 2, 1, 3):
+            cols = slice(CW * c, CW * (c + 1))
+            nc.vector.quantize_mx(out=y_codes[:, cols].bitcast(FP8X4), scales=y_scales[:, cols],
+                                  in_=y_bf[c][:].rearrange("p t j -> p (t j)"))
+        for half in range(2):
+            cols = slice(T // 2 * half, T // 2 * (half + 1))
+            nc.sync.dma_start(words_v[:, cols], y_codes[:, cols].bitcast(I32))
+        for g in range(4):
+            nc.scalar.dma_start(out_2[0, 4 * g : 4 * g + 4, :].bitcast(I32), y_scales[32 * g : 32 * g + 4, :].bitcast(I32))

@@ -1,6 +1,7 @@
 from contextlib import ExitStack
 
 import concourse.mybir as mybir
+from concourse.masks import make_identity
 
 D, T, I, Q = 512, 1024, 256, 512
 FLOPS = 2 * D * Q * I * 2
@@ -28,7 +29,17 @@ def tile_attend_bmassmerge_pl_kernel(tc, query, keys, mass, target, qs, qrows, o
     with ExitStack() as ctx:
         lists = ctx.enter_context(tc.tile_pool(name="lists", bufs=1))
         sb = ctx.enter_context(tc.tile_pool(name="sb", bufs=1))
+        reuse = ctx.enter_context(tc.tile_pool(name="reuse", bufs=1))
         ps = ctx.enter_context(tc.psum_pool(name="ps", bufs=1))
+
+        def bank(number, shape, name):
+            return ps.tile(shape, F32, name=name, tag="bank%d" % number)
+
+        ident = sb.tile([P, P], F32, name="ident")
+        make_identity(nc, ident[:])
+
+        def turn(dst, src, start=True, stop=True):
+            nc.tensor.matmul(dst, src, ident[:], start=start, stop=stop, is_transpose=True)
 
         list_t = [lists.tile([P, I // 16], U16, name="list%d" % n) for n in range(2)]
         nc.sync.dma_start(list_t[0][:], offs)
@@ -41,15 +52,15 @@ def tile_attend_bmassmerge_pl_kernel(tc, query, keys, mass, target, qs, qrows, o
         for j in range(PACK):
             nc.sync.dma_start(key_t[j][:], keys_v[:, j, :])
 
-        def load_halves(src, name):
+        def load_halves(src, halves):
             view = src.rearrange("(p j) c -> p j c", j=PACK)
-            halves = [sb.tile([P, PACK, 256], F32, name="%s%d" % (name, h)) for h in range(2)]
             for h in range(2):
                 nc.sync.dma_start(halves[h][:], view[:, :, 256 * h : 256 * (h + 1)])
             return halves
 
-        query_h = load_halves(query, "query_raw")
-        qrows_h = load_halves(qrows, "qrows_raw")
+        query_h = load_halves(query, [sb.tile([P, PACK, 256], F32, name="query_raw0"),
+                                      reuse.tile([P, PACK, 256], F32, name="query_raw1", offset=0)])
+        qrows_h = load_halves(qrows, [sb.tile([P, PACK, 256], F32, name="qrows_raw%d" % h) for h in range(2)])
         qs_t = sb.tile([P, PACK], F32, name="qs_t")
         nc.sync.dma_start(qs_t[:], qs.rearrange("(s r) o -> s (r o)", r=PACK))
         target_t = sb.tile([P, PACK, I], F32, name="target_t")
@@ -67,12 +78,32 @@ def tile_attend_bmassmerge_pl_kernel(tc, query, keys, mass, target, qs, qrows, o
         m12 = sb.tile([P, 2, I], F32, name="m12")
         for n in range(2):
             nc.vector.tensor_copy(m12[:, n, :], mass_t[:].indirect(list_t[n][:]))
-        msum = sb.tile([P, I], F32, name="msum")
-        nc.vector.tensor_tensor(msum[:], m12[:, 0, :], m12[:, 1, :], ALU.add)
+        msum_ps = bank(1, [P, 2, P], "msum_ps")
+        for h in range(2):
+            for n in range(2):
+                turn(msum_ps[:, h, :], m12[:, n, P * h : P * (h + 1)], start=(n == 0), stop=(n == 1))
+        m_ps = bank(0, [P, 2, 2, P], "m_ps")
+        for n in range(2):
+            for h in range(2):
+                turn(m_ps[:, n, h, :], m12[:, n, P * h : P * (h + 1)])
+        rcol = sb.tile([P, 2], F32, name="rcol")
+        nc.vector.reciprocal(rcol[:], msum_ps[:, :, 0])
+        lncol = sb.tile([P, 2], F32, name="lncol")
+        nc.scalar.activation(lncol[:], msum_ps[:, :, 0], ACT.Ln)
+        sharecol = sb.tile([P, 2, 2], F32, name="sharecol")
+        for h in range(2):
+            nc.scalar.activation(sharecol[:, :, h], m_ps[:, :, h, 0], ACT.Copy, scale=rcol[:, h : h + 1])
+        ln_ps = bank(3, [P, 2, P], "ln_ps")
+        for h in range(2):
+            turn(ln_ps[:, h, :], lncol[:, h : h + 1].to_broadcast([P, P]))
+        share_ps = bank(2, [P, 2, 2, P], "share_ps")
+        for n in range(2):
+            for h in range(2):
+                turn(share_ps[:, n, h, :], sharecol[:, n, h : h + 1].to_broadcast([P, P]))
         lnm = sb.tile([P, I], F32, name="lnm")
-        nc.scalar.activation(lnm[:], msum[:], ACT.Ln)
-        seed = sb.tile([P, I], F32, name="seed")
-        nc.scalar.activation(seed[:], lnm[:], ACT.Exp, scale=-1.0)
+        nc.scalar.copy(lnm[:], ln_ps[:].rearrange("p h i -> p (h i)"))
+        share = sb.tile([P, 2, I], F32, name="share")
+        nc.scalar.copy(share[:], share_ps[:].rearrange("p n h i -> p n (h i)"))
 
         def deal(halves, name):
             dealt = sb.tile([P, PACK, P, PACK], BF16, name=name + "_bf", align_bytes=64)
@@ -90,35 +121,33 @@ def tile_attend_bmassmerge_pl_kernel(tc, query, keys, mass, target, qs, qrows, o
             return codes, scales
 
         query_bf = deal(query_h, "query")
-        qrows_bf = deal(qrows_h, "qrows")
-        tq = sb.tile([P, PACK, I], F32, name="tq")
-        for r in range(PACK):
-            nc.scalar.activation(tq[:, r, :], target_t[:, r, :], ACT.Copy, scale=qs_t[:, r : r + 1])
 
-        wk = [sb.tile([P, PACK, I], F32, name="wk%d" % n) for n in range(2)]
-        resid = sb.tile([P, I], F32, name="resid")
-        rinv = sb.tile([P, I], F32, name="rinv")
-        for j in range(PACK):
-            for n in range(2):
-                nc.vector.tensor_tensor(wk[n][:, j, :], key_t[j][:].indirect(list_t[n][:]), m12[:, n, :], ALU.mult)
-            if j == 2:
-                nc.vector.scalar_tensor_tensor(resid[:], msum[:], -1.0, seed[:], ALU.mult, ALU.mult)
-        nc.vector.scalar_tensor_tensor(rinv[:], resid[:], 2.0, seed[:], ALU.add, ALU.mult)
-        ksum = sb.tile([P, PACK, I], F32, name="ksum")
-        nc.vector.tensor_tensor(ksum[:], wk[0][:], wk[1][:], ALU.add)
+        wk = [[sb.tile([P, I], F32, name="wk%d_%d" % (n, j)) for j in range(PACK)] for n in range(2)]
+        km_back = [bank(h, [P, 2, P], "km_back%d" % h) for h in range(2)]
+        for u in range(2):
+            km_ps = [bank(4 + 2 * u + h, [P, 2, P], "km_ps%d_%d" % (u, h)) for h in range(2)]
+            for e in range(2):
+                j = 2 * u + e
+                for n in range(2):
+                    nc.vector.tensor_tensor(wk[n][j][:], key_t[j][:].indirect(list_t[n][:]), m12[:, n, :], ALU.mult)
+                    for h in range(2):
+                        turn(km_ps[h][:, e, :], wk[n][j][:, P * h : P * (h + 1)], start=(n == 0), stop=(n == 1))
+            for h in range(2):
+                if u == 0:
+                    pairs = sb.tile([P, P, 2], BF16, name="pairs0_%d" % h)
+                else:
+                    pairs = reuse.tile([P, P, 2], BF16, name="pairs1_%d" % h, offset=512 * h)
+                nc.scalar.activation(pairs[:], km_ps[h][:].rearrange("i e p -> i p e"), ACT.Copy, scale=rcol[:, h : h + 1])
+                turn(km_back[h][:, u, :], pairs[:].rearrange("i p e -> i (p e)").bitcast(F32))
         q_codes, q_scales = quantise(query_bf[:].rearrange("p r s j -> p (r s j)"), Q, "query")
-        km_bf = sb.tile([P, I, PACK], BF16, name="km_bf", align_bytes=64)
-        nc.vector.tensor_tensor(
-            km_bf[:].rearrange("p (c i) j -> p c j i", i=RUN),
-            ksum[:].rearrange("p j (c i) -> p c j i", i=RUN),
-            rinv[:].rearrange("p (c i) -> p c i", i=RUN).unsqueeze(2).to_broadcast([P, I // RUN, PACK, RUN]),
-            ALU.mult,
-        )
-        share = sb.tile([P, 2, I], F32, name="share")
-        nc.vector.tensor_tensor(share[:], m12[:], rinv[:].unsqueeze(1).to_broadcast([P, 2, I]), ALU.mult)
-        km_codes, km_scales = quantise(km_bf[:].rearrange("p i j -> p (i j)"), I, "km")
+        km_bf = sb.tile([P, I * PACK], BF16, name="km_bf", align_bytes=64)
+        km_words = km_bf[:].bitcast(F32).rearrange("p (h i u) -> p h i u", h=2, u=2)
+        for h in range(2):
+            nc.vector.tensor_copy(km_words[:, h, :, :], km_back[h][:].rearrange("p u i -> p i u"))
+        qrows_bf = deal(qrows_h, "qrows")
+        km_codes, km_scales = quantise(km_bf[:], I, "km")
 
-        score = [ps.tile([P, 2, I], F32, name="score%d" % h) for h in range(2)]
+        score = [bank(h, [P, 2, I], "score%d" % h) for h in range(2)]
         for r in range(PACK):
             cols = slice(P * r, P * (r + 1))
             nc.tensor.matmul_mx(
@@ -127,7 +156,20 @@ def tile_attend_bmassmerge_pl_kernel(tc, query, keys, mass, target, qs, qrows, o
                 rhs=km_codes[:].bitcast(FP8X4), rhs_scale=km_scales[:],
                 start=True, stop=True,
             )
-        r_codes, r_scales = quantise(qrows_bf[:].rearrange("p r s j -> p (r s j)"), D, "qrows")
+
+        BLOCKS = T // P
+
+        def open_sum(j, first_bank):
+            banks = [bank(first_bank + g, [P, 4, P], "yt_ps%d_%d" % (j, g)) for g in range(2)]
+            turn_in(banks, old_t[j], True, False)
+            return banks
+
+        def turn_in(banks, src, start, stop):
+            for b in range(BLOCKS):
+                turn(banks[b // 4][:, b % 4, :], src[:, P * b : P * (b + 1)],
+                     start=(start and b % 4 == 0), stop=(stop and b % 4 == 3))
+
+        yt_ps = [open_sum(0, 2), open_sum(1, 4)]
 
         s_t = [sb.tile([P, 2, I], F32, name="s%d" % h) for h in range(2)]
         negmax = [sb.tile([P, 2], F32, name="negmax%d" % h) for h in range(2)]
@@ -146,21 +188,23 @@ def tile_attend_bmassmerge_pl_kernel(tc, query, keys, mass, target, qs, qrows, o
             nc.vector.reciprocal(rowinv[h][:], rowsum[h][:])
             for e in range(2):
                 r = 2 * h + e
-                nc.vector.tensor_scalar(pn[:, r, :], p_t[h][:, e, :], rowinv[h][:, e : e + 1], qs_t[:, r : r + 1],
-                                        ALU.mult, ALU.mult)
+                nc.vector.scalar_tensor_tensor(pn[:, r, :], p_t[h][:, e, :], rowinv[h][:, e : e + 1], target_t[:, r, :],
+                                               ALU.mult, ALU.subtract)
+            if h == 0:
+                r_codes, r_scales = quantise(qrows_bf[:].rearrange("p r s j -> p (r s j)"), D, "qrows")
         ds_bf = sb.tile([P, I, PACK], BF16, name="ds_bf", align_bytes=64)
         nc.vector.tensor_tensor(
             ds_bf[:].rearrange("p (c i) r -> p c r i", i=RUN),
             pn[:].rearrange("p r (c i) -> p c r i", i=RUN),
-            tq[:].rearrange("p r (c i) -> p c r i", i=RUN),
-            ALU.subtract,
+            qs_t[:].unsqueeze(1).unsqueeze(3).to_broadcast([P, I // RUN, PACK, RUN]),
+            ALU.mult,
         )
         ds_codes, ds_scales = quantise(ds_bf[:].rearrange("p i r -> p (i r)"), I, "ds")
 
         gk = []
         for j in range(PACK):
             cols = slice(P * j, P * (j + 1))
-            acc = ps.tile([P, I], F32, name="gk_acc%d" % j)
+            acc = bank((6 + j) % 8, [P, I], "gk_acc%d" % j)
             nc.tensor.matmul_mx(
                 out=acc[:],
                 lhsT=r_codes[:, cols].bitcast(FP8X4), lhsT_scale=r_scales[:, cols],
@@ -171,57 +215,69 @@ def tile_attend_bmassmerge_pl_kernel(tc, query, keys, mass, target, qs, qrows, o
             nc.scalar.copy(gk[j][:], acc[:])
 
         out_v = out_0.rearrange("(p j) t -> p j t", j=PACK)
-        y = [sb.tile([P, 2, T], F32, name="y%d" % u) for u in range(2)]
+        y = sb.tile([P, PACK, T], F32, name="y")
         y_bf = [sb.tile([P, CW, PACK], BF16, name="y_bf%d" % c, align_bytes=64) for c in range(CHUNKS)]
 
         def scatter(n, j):
             nc.vector.tensor_tensor(win[n][j % 2][:].indirect(list_t[n][:]), gk[j][:], share[:, n, :], ALU.mult)
 
-        def add_first(j):
-            nc.vector.tensor_tensor(y[j // 2][:, j % 2, :], old_t[j][:], win[0][j % 2][:], ALU.add)
-
-        def add_second(j, cols):
-            dst = y[j // 2][:, j % 2, cols]
-            nc.vector.tensor_tensor(dst, dst, win[1][j % 2][:, cols], ALU.add)
-
-        def weave(u, c, on_scalar):
-            dst = y_bf[c][:, :, 2 * u : 2 * u + 2].rearrange("p (c i) j -> p c j i", i=RUN)
-            src = y[u][:, :, CW * c : CW * (c + 1)].rearrange("p j (c i) -> p c j i", i=RUN)
+        def weave(first, last, c, on_scalar):
+            dst = y_bf[c][:, :, first:last].rearrange("p (c i) j -> p c j i", i=RUN)
+            src = y[:, first:last, CW * c : CW * (c + 1)].rearrange("p j (c i) -> p c j i", i=RUN)
             if on_scalar:
                 nc.scalar.copy(dst, src)
             else:
                 nc.vector.tensor_copy(dst, src)
 
-        whole = slice(0, T)
-        for j in range(PACK):
-            scatter(0, j)
-            if j > 0:
-                add_second(j - 1, whole)
-                nc.sync.dma_start(out_v[:, j - 1, :], y[(j - 1) // 2][:, (j - 1) % 2, :])
-            if j == 2:
-                for c in range(CHUNKS):
-                    weave(0, c, True)
-            scatter(1, j)
-            add_first(j)
+        def turn_back(j, first_bank):
+            yt = [sb.tile([P, 4, P], F32, name="yt%d_%d" % (j, g)) for g in range(2)]
+            for g in range(2):
+                nc.scalar.copy(yt[g][:], yt_ps[j][g][:])
+            back = []
+            for g in range(2):
+                back.append(bank(first_bank + g, [P, 4, P], "back%d_%d" % (j, g)))
+                for b in range(4):
+                    turn(back[g][:, b, :], yt[g][:, b, :])
+            return [tile[:].rearrange("p b t -> p (b t)") for tile in back]
+
+        halves = [slice(512 * g, 512 * (g + 1)) for g in range(2)]
+        for j in range(2):
+            for n in range(2):
+                scatter(n, j)
+                turn_in(yt_ps[j], win[n][j], False, n == 1)
+            back = turn_back(j, (6 + 2 * j) % 8)
+            for g in range(2):
+                nc.scalar.copy(y[:, j, halves[g]], back[g])
+            nc.sync.dma_start(out_v[:, j, :], y[:, j, :])
+            for c in range(CHUNKS):
+                if (c < 2) == (j == 0):
+                    weave(0, j + 1, c, True)
+        scatter(0, 2)
+        scatter(1, 2)
+        nc.vector.tensor_tensor(y[:, 2, :], old_t[2][:], win[0][0][:], ALU.add)
+        scatter(0, 3)
+        nc.vector.tensor_tensor(y[:, 2, :], y[:, 2, :], win[1][0][:], ALU.add)
+        nc.sync.dma_start(out_v[:, 2, :], y[:, 2, :])
+        scatter(1, 3)
+        nc.vector.tensor_tensor(y[:, 3, :], old_t[3][:], win[0][1][:], ALU.add)
 
         y_codes = sb.tile([P, T], U32, name="y_codes", align_bytes=64)
         y_scales = sb.tile([P, T], U8, name="y_scales", align_bytes=64)
         words_v = out_1[0].rearrange("l c r -> l (c r)").bitcast(I32)
         for c in range(CHUNKS):
-            add_second(PACK - 1, slice(CW * c, CW * (c + 1)))
+            cols = slice(CW * c, CW * (c + 1))
+            nc.vector.tensor_tensor(y[:, 3, cols], y[:, 3, cols], win[1][1][:, cols], ALU.add)
             if c < 2:
-                weave(1, c, True)
+                weave(1, PACK, c, True)
             if c % 2 == 1:
-                half = slice(CW * (c - 1), CW * (c + 1))
-                nc.sync.dma_start(out_v[:, PACK - 1, half], y[1][:, 1, half])
+                nc.sync.dma_start(out_v[:, 3, halves[c // 2]], y[:, 3, halves[c // 2]])
         for c in (2, 3):
-            weave(1, c, False)
-        for c in (0, 2, 1, 3):
+            weave(2, PACK, c, False)
+        for c in range(CHUNKS):
             cols = slice(CW * c, CW * (c + 1))
             nc.vector.quantize_mx(out=y_codes[:, cols].bitcast(FP8X4), scales=y_scales[:, cols],
                                   in_=y_bf[c][:].rearrange("p t j -> p (t j)"))
-        for half in range(2):
-            cols = slice(T // 2 * half, T // 2 * (half + 1))
-            nc.sync.dma_start(words_v[:, cols], y_codes[:, cols].bitcast(I32))
+            if c % 2 == 1:
+                nc.sync.dma_start(words_v[:, halves[c // 2]], y_codes[:, halves[c // 2]].bitcast(I32))
         for g in range(4):
             nc.scalar.dma_start(out_2[0, 4 * g : 4 * g + 4, :].bitcast(I32), y_scales[32 * g : 32 * g + 4, :].bitcast(I32))

@@ -29,7 +29,6 @@ def tile_attend_bmassmerge_pl_kernel(tc, query, keys, mass, target, qs, qrows, o
     with ExitStack() as ctx:
         lists = ctx.enter_context(tc.tile_pool(name="lists", bufs=1))
         sb = ctx.enter_context(tc.tile_pool(name="sb", bufs=1))
-        reuse = ctx.enter_context(tc.tile_pool(name="reuse", bufs=1))
         ps = ctx.enter_context(tc.psum_pool(name="ps", bufs=1))
 
         def bank(number, shape, name):
@@ -41,12 +40,12 @@ def tile_attend_bmassmerge_pl_kernel(tc, query, keys, mass, target, qs, qrows, o
         def turn(dst, src, start=True, stop=True):
             nc.tensor.matmul(dst, src, ident[:], start=start, stop=stop, is_transpose=True)
 
+        mass_t = sb.tile([P, T], F32, name="mass_t")
+        nc.sync.dma_start(mass_t[:], mass)
         list_t = [lists.tile([P, I // 16], U16, name="list%d" % n) for n in range(2)]
         nc.sync.dma_start(list_t[0][:], offs)
         nc.sync.dma_start(list_t[1][:], offs2)
 
-        mass_t = sb.tile([P, T], F32, name="mass_t")
-        nc.sync.dma_start(mass_t[:], mass)
         keys_v = keys.rearrange("(p j) t -> p j t", j=PACK)
         key_t = [sb.tile([P, T], F32, name="key%d" % j) for j in range(PACK)]
         for j in range(PACK):
@@ -58,8 +57,7 @@ def tile_attend_bmassmerge_pl_kernel(tc, query, keys, mass, target, qs, qrows, o
                 nc.sync.dma_start(halves[h][:], view[:, :, 256 * h : 256 * (h + 1)])
             return halves
 
-        query_h = load_halves(query, [sb.tile([P, PACK, 256], F32, name="query_raw0"),
-                                      reuse.tile([P, PACK, 256], F32, name="query_raw1", offset=0)])
+        query_h = load_halves(query, [sb.tile([P, PACK, 256], F32, name="query_raw%d" % h) for h in range(2)])
         qrows_h = load_halves(qrows, [sb.tile([P, PACK, 256], F32, name="qrows_raw%d" % h) for h in range(2)])
         qs_t = sb.tile([P, PACK], F32, name="qs_t")
         nc.sync.dma_start(qs_t[:], qs.rearrange("(s r) o -> s (r o)", r=PACK))
@@ -86,10 +84,10 @@ def tile_attend_bmassmerge_pl_kernel(tc, query, keys, mass, target, qs, qrows, o
         for n in range(2):
             for h in range(2):
                 turn(m_ps[:, n, h, :], m12[:, n, P * h : P * (h + 1)])
-        rcol = sb.tile([P, 2], F32, name="rcol")
-        nc.vector.reciprocal(rcol[:], msum_ps[:, :, 0])
         lncol = sb.tile([P, 2], F32, name="lncol")
         nc.scalar.activation(lncol[:], msum_ps[:, :, 0], ACT.Ln)
+        rcol = sb.tile([P, 2], F32, name="rcol")
+        nc.vector.reciprocal(rcol[:], msum_ps[:, :, 0])
         sharecol = sb.tile([P, 2, 2], F32, name="sharecol")
         for h in range(2):
             nc.scalar.activation(sharecol[:, :, h], m_ps[:, :, h, 0], ACT.Copy, scale=rcol[:, h : h + 1])
@@ -105,10 +103,10 @@ def tile_attend_bmassmerge_pl_kernel(tc, query, keys, mass, target, qs, qrows, o
         share = sb.tile([P, 2, I], F32, name="share")
         nc.scalar.copy(share[:], share_ps[:].rearrange("p n h i -> p n (h i)"))
 
-        def deal(halves, name):
+        def deal(halves, name, copies):
             dealt = sb.tile([P, PACK, P, PACK], BF16, name=name + "_bf", align_bytes=64)
             for h in range(2):
-                nc.scalar.copy(
+                copies[h](
                     dealt[:, :, 64 * h : 64 * (h + 1), :].rearrange("p r s j -> p s j r"),
                     halves[h][:].rearrange("p j (s r) -> p s j r", r=PACK),
                 )
@@ -120,7 +118,6 @@ def tile_attend_bmassmerge_pl_kernel(tc, query, keys, mass, target, qs, qrows, o
             nc.vector.quantize_mx(out=codes[:].bitcast(FP8X4), scales=scales[:], in_=src_flat)
             return codes, scales
 
-        query_bf = deal(query_h, "query")
 
         wk = [[sb.tile([P, I], F32, name="wk%d_%d" % (n, j)) for j in range(PACK)] for n in range(2)]
         km_back = [bank(h, [P, 2, P], "km_back%d" % h) for h in range(2)]
@@ -133,18 +130,19 @@ def tile_attend_bmassmerge_pl_kernel(tc, query, keys, mass, target, qs, qrows, o
                     for h in range(2):
                         turn(km_ps[h][:, e, :], wk[n][j][:, P * h : P * (h + 1)], start=(n == 0), stop=(n == 1))
             for h in range(2):
-                if u == 0:
-                    pairs = sb.tile([P, P, 2], BF16, name="pairs0_%d" % h)
-                else:
-                    pairs = reuse.tile([P, P, 2], BF16, name="pairs1_%d" % h, offset=512 * h)
+                pairs = sb.tile([P, P, 2], BF16, name="pairs%d_%d" % (u, h))
                 nc.scalar.activation(pairs[:], km_ps[h][:].rearrange("i e p -> i p e"), ACT.Copy, scale=rcol[:, h : h + 1])
                 turn(km_back[h][:, u, :], pairs[:].rearrange("i p e -> i (p e)").bitcast(F32))
+        query_bf = deal(query_h, "query", [nc.scalar.copy, nc.vector.tensor_copy])
         q_codes, q_scales = quantise(query_bf[:].rearrange("p r s j -> p (r s j)"), Q, "query")
         km_bf = sb.tile([P, I * PACK], BF16, name="km_bf", align_bytes=64)
         km_words = km_bf[:].bitcast(F32).rearrange("p (h i u) -> p h i u", h=2, u=2)
-        for h in range(2):
-            nc.vector.tensor_copy(km_words[:, h, :, :], km_back[h][:].rearrange("p u i -> p i u"))
-        qrows_bf = deal(qrows_h, "qrows")
+        for h, copy in enumerate([nc.vector.tensor_copy, nc.scalar.copy]):
+            copy(km_words[:, h, :, :], km_back[h][:].rearrange("p u i -> p i u"))
+        qrows_bf = deal(qrows_h, "qrows", [nc.scalar.copy, nc.scalar.copy])
+        tq = sb.tile([P, PACK, I], F32, name="tq")
+        for r in range(PACK):
+            nc.gpsimd.tensor_scalar(tq[:, r, :], target_t[:, r, :], qs_t[:, r : r + 1], 0.0, ALU.mult, ALU.add)
         km_codes, km_scales = quantise(km_bf[:], I, "km")
 
         score = [bank(h, [P, 2, I], "score%d" % h) for h in range(2)]
@@ -172,42 +170,41 @@ def tile_attend_bmassmerge_pl_kernel(tc, query, keys, mass, target, qs, qrows, o
         yt_ps = [open_sum(0, 2), open_sum(1, 4)]
 
         s_t = [sb.tile([P, 2, I], F32, name="s%d" % h) for h in range(2)]
-        negmax = [sb.tile([P, 2], F32, name="negmax%d" % h) for h in range(2)]
+        negmax = [sb.tile([P, 1], F32, name="negmax%d" % r) for r in range(PACK)]
         rowsum = [sb.tile([P, 2], F32, name="rowsum%d" % h) for h in range(2)]
         rowinv = [sb.tile([P, 2], F32, name="rowinv%d" % h) for h in range(2)]
-        p_t = [sb.tile([P, 2, I], F32, name="p%d" % h) for h in range(2)]
+        p_t = [sb.tile([P, I], F32, name="p%d" % r) for r in range(PACK)]
         pn = sb.tile([P, PACK, I], F32, name="pn")
         for h in range(2):
             nc.vector.tensor_tensor(s_t[h][:], score[h][:], lnm[:].unsqueeze(1).to_broadcast([P, 2, I]), ALU.add)
-        for h in range(2):
-            nc.vector.tensor_reduce(negmax[h][:], s_t[h][:], AX.X, ALU.max, negate=True)
-            for e in range(2):
-                nc.scalar.activation(p_t[h][:, e, :], s_t[h][:, e, :], ACT.Exp,
-                                     bias=negmax[h][:, e : e + 1], accum_out=rowsum[h][:, e : e + 1])
+        for r in range(PACK):
+            h, e = divmod(r, 2)
+            nc.vector.tensor_reduce(negmax[r][:], s_t[h][:, e, :], AX.X, ALU.max, negate=True)
+            nc.scalar.activation(p_t[r][:], s_t[h][:, e, :], ACT.Exp, bias=negmax[r][:], accum_out=rowsum[h][:, e : e + 1])
         for h in range(2):
             nc.vector.reciprocal(rowinv[h][:], rowsum[h][:])
             for e in range(2):
                 r = 2 * h + e
-                nc.vector.scalar_tensor_tensor(pn[:, r, :], p_t[h][:, e, :], rowinv[h][:, e : e + 1], target_t[:, r, :],
-                                               ALU.mult, ALU.subtract)
-            if h == 0:
-                r_codes, r_scales = quantise(qrows_bf[:].rearrange("p r s j -> p (r s j)"), D, "qrows")
+                nc.vector.tensor_scalar(pn[:, r, :], p_t[r][:], rowinv[h][:, e : e + 1], qs_t[:, r : r + 1],
+                                        ALU.mult, ALU.mult)
         ds_bf = sb.tile([P, I, PACK], BF16, name="ds_bf", align_bytes=64)
         nc.vector.tensor_tensor(
             ds_bf[:].rearrange("p (c i) r -> p c r i", i=RUN),
             pn[:].rearrange("p r (c i) -> p c r i", i=RUN),
-            qs_t[:].unsqueeze(1).unsqueeze(3).to_broadcast([P, I // RUN, PACK, RUN]),
-            ALU.mult,
+            tq[:].rearrange("p r (c i) -> p c r i", i=RUN),
+            ALU.subtract,
         )
+        r_quant = [quantise(qrows_bf[:, 0, :, :].rearrange("p s j -> p (s j)"), P, "qrows0")]
         ds_codes, ds_scales = quantise(ds_bf[:].rearrange("p i r -> p (i r)"), I, "ds")
 
         gk = []
         for j in range(PACK):
-            cols = slice(P * j, P * (j + 1))
+            if j > 0:
+                r_quant.append(quantise(qrows_bf[:, j, :, :].rearrange("p s j -> p (s j)"), P, "qrows%d" % j))
             acc = bank((6 + j) % 8, [P, I], "gk_acc%d" % j)
             nc.tensor.matmul_mx(
                 out=acc[:],
-                lhsT=r_codes[:, cols].bitcast(FP8X4), lhsT_scale=r_scales[:, cols],
+                lhsT=r_quant[j][0][:].bitcast(FP8X4), lhsT_scale=r_quant[j][1][:],
                 rhs=ds_codes[:].bitcast(FP8X4), rhs_scale=ds_scales[:],
                 start=True, stop=True,
             )
@@ -241,25 +238,33 @@ def tile_attend_bmassmerge_pl_kernel(tc, query, keys, mass, target, qs, qrows, o
             return [tile[:].rearrange("p b t -> p (b t)") for tile in back]
 
         halves = [slice(512 * g, 512 * (g + 1)) for g in range(2)]
-        for j in range(2):
-            for n in range(2):
-                scatter(n, j)
-                turn_in(yt_ps[j], win[n][j], False, n == 1)
-            back = turn_back(j, (6 + 2 * j) % 8)
+        yt_ps.append(open_sum(2, 6))
+        def finish(j, back):
             for g in range(2):
                 nc.scalar.copy(y[:, j, halves[g]], back[g])
-            nc.sync.dma_start(out_v[:, j, :], y[:, j, :])
-            for c in range(CHUNKS):
-                if (c < 2) == (j == 0):
-                    weave(0, j + 1, c, True)
+            nc.scalar.dma_start(out_v[:, j, :], y[:, j, :])
+
+        for n in range(2):
+            scatter(n, 0)
+            turn_in(yt_ps[0], win[n][0], False, n == 1)
+        finish(0, turn_back(0, 0))
+        for n in range(2):
+            scatter(n, 1)
+            turn_in(yt_ps[1], win[n][1], False, n == 1)
+        back1 = turn_back(1, 2)
         scatter(0, 2)
+        turn_in(yt_ps[2], win[0][0], False, True)
+        back = turn_back(2, 0)
+        finish(1, back1)
+        for c in range(CHUNKS):
+            weave(0, 1 if c < 2 else 2, c, True)
         scatter(1, 2)
-        nc.vector.tensor_tensor(y[:, 2, :], old_t[2][:], win[0][0][:], ALU.add)
         scatter(0, 3)
-        nc.vector.tensor_tensor(y[:, 2, :], y[:, 2, :], win[1][0][:], ALU.add)
-        nc.sync.dma_start(out_v[:, 2, :], y[:, 2, :])
         scatter(1, 3)
         nc.vector.tensor_tensor(y[:, 3, :], old_t[3][:], win[0][1][:], ALU.add)
+        for g in range(2):
+            nc.vector.tensor_tensor(y[:, 2, halves[g]], back[g], win[1][0][:, halves[g]], ALU.add)
+        nc.sync.dma_start(out_v[:, 2, :], y[:, 2, :])
 
         y_codes = sb.tile([P, T], U32, name="y_codes", align_bytes=64)
         y_scales = sb.tile([P, T], U8, name="y_scales", align_bytes=64)
@@ -280,4 +285,4 @@ def tile_attend_bmassmerge_pl_kernel(tc, query, keys, mass, target, qs, qrows, o
             if c % 2 == 1:
                 nc.sync.dma_start(words_v[:, halves[c // 2]], y_codes[:, halves[c // 2]].bitcast(I32))
         for g in range(4):
-            nc.scalar.dma_start(out_2[0, 4 * g : 4 * g + 4, :].bitcast(I32), y_scales[32 * g : 32 * g + 4, :].bitcast(I32))
+            (nc.scalar if g < 2 else nc.sync).dma_start(out_2[0, 4 * g : 4 * g + 4, :].bitcast(I32), y_scales[32 * g : 32 * g + 4, :].bitcast(I32))

@@ -58,7 +58,8 @@ def tile_attend_bmassmerge_pl_kernel(tc, query, keys, mass, target, qs, qrows, o
             return halves
 
         query_h = load_halves(query, [sb.tile([P, PACK, 256], F32, name="query_raw%d" % h) for h in range(2)])
-        qrows_h = load_halves(qrows, [sb.tile([P, PACK, 256], F32, name="qrows_raw%d" % h) for h in range(2)])
+        qrows_raw = sb.tile([P, PACK, D], F32, name="qrows_raw")
+        nc.sync.dma_start(qrows_raw[:], qrows.rearrange("(p j) c -> p j c", j=PACK))
         qs_t = sb.tile([P, PACK], F32, name="qs_t")
         nc.sync.dma_start(qs_t[:], qs.rearrange("(s r) o -> s (r o)", r=PACK))
         target_t = sb.tile([P, PACK, I], F32, name="target_t")
@@ -71,7 +72,7 @@ def tile_attend_bmassmerge_pl_kernel(tc, query, keys, mass, target, qs, qrows, o
         win = [[sb.tile([P, T], F32, name="win%d_%d" % (n, b)) for b in range(2)] for n in range(2)]
         for b in range(2):
             for n in range(2):
-                nc.vector.memset(win[n][b][:], 0.0)
+                (nc.gpsimd if n + b == 2 else nc.vector).memset(win[n][b][:], 0.0)
 
         m12 = sb.tile([P, 2, I], F32, name="m12")
         for n in range(2):
@@ -126,24 +127,38 @@ def tile_attend_bmassmerge_pl_kernel(tc, query, keys, mass, target, qs, qrows, o
             for e in range(2):
                 j = 2 * u + e
                 for n in range(2):
-                    nc.vector.tensor_tensor(wk[n][j][:], key_t[j][:].indirect(list_t[n][:]), m12[:, n, :], ALU.mult)
+                    last = j == PACK - 1 and n == 1
+                    if not last:
+                        nc.vector.tensor_tensor(wk[n][j][:], key_t[j][:].indirect(list_t[n][:]), m12[:, n, :], ALU.mult)
                     for h in range(2):
+                        if last:
+                            nc.vector.tensor_tensor(wk[n][j][:, P * h : P * (h + 1)],
+                                                    key_t[j][:].indirect(list_t[n][:, 8 * h : 8 * (h + 1)]),
+                                                    m12[:, n, P * h : P * (h + 1)], ALU.mult)
                         turn(km_ps[h][:, e, :], wk[n][j][:, P * h : P * (h + 1)], start=(n == 0), stop=(n == 1))
             for h in range(2):
-                pairs = sb.tile([P, P, 2], BF16, name="pairs%d_%d" % (u, h))
+                tag = "qrows_then_tq" if u + h == 2 else "pairs%d_%d" % (u, h)
+                pairs = sb.tile([P, P, 2], BF16, name="pairs%d_%d" % (u, h), tag=tag, align_bytes=64)
                 nc.scalar.activation(pairs[:], km_ps[h][:].rearrange("i e p -> i p e"), ACT.Copy, scale=rcol[:, h : h + 1])
                 turn(km_back[h][:, u, :], pairs[:].rearrange("i p e -> i (p e)").bitcast(F32))
         query_bf = deal(query_h, "query", [nc.scalar.copy, nc.vector.tensor_copy])
         q_codes, q_scales = quantise(query_bf[:].rearrange("p r s j -> p (r s j)"), Q, "query")
         km_bf = sb.tile([P, I * PACK], BF16, name="km_bf", align_bytes=64)
         km_words = km_bf[:].bitcast(F32).rearrange("p (h i u) -> p h i u", h=2, u=2)
-        for h, copy in enumerate([nc.vector.tensor_copy, nc.scalar.copy]):
-            copy(km_words[:, h, :, :], km_back[h][:].rearrange("p u i -> p i u"))
-        qrows_bf = deal(qrows_h, "qrows", [nc.scalar.copy, nc.scalar.copy])
-        tq = sb.tile([P, PACK, I], F32, name="tq")
+        for h in range(2):
+            nc.vector.tensor_copy(km_words[:, h, :, :], km_back[h][:].rearrange("p u i -> p i u"))
+        km_codes, km_scales = quantise(km_bf[:], I, "km")
+
+        def quantise_qrows(u, tag):
+            dealt = sb.tile([P, 2, P, PACK], BF16, name="qrows_bf%d" % u, tag=tag, align_bytes=64)
+            nc.scalar.copy(dealt[:].rearrange("p e m j -> p m j e"),
+                           qrows_raw[:].rearrange("p j (m t) -> p m j t", t=PACK)[:, :, :, 2 * u : 2 * u + 2])
+            return quantise(dealt[:].rearrange("p e m j -> p (e m j)"), 2 * P, "qrows%d" % u)
+
+        r_quant = [quantise_qrows(0, "qrows_then_tq")]
+        tq = sb.tile([P, PACK, I], F32, name="tq", tag="qrows_then_tq", align_bytes=64)
         for r in range(PACK):
             nc.gpsimd.tensor_scalar(tq[:, r, :], target_t[:, r, :], qs_t[:, r : r + 1], 0.0, ALU.mult, ALU.add)
-        km_codes, km_scales = quantise(km_bf[:], I, "km")
 
         score = [bank(h, [P, 2, I], "score%d" % h) for h in range(2)]
         for r in range(PACK):
@@ -169,7 +184,7 @@ def tile_attend_bmassmerge_pl_kernel(tc, query, keys, mass, target, qs, qrows, o
 
         yt_ps = [open_sum(0, 2), open_sum(1, 4)]
 
-        s_t = [sb.tile([P, 2, I], F32, name="s%d" % h) for h in range(2)]
+        s_t = [sb.tile([P, 2, I], F32, name="s%d" % h, tag="s%d" % h, align_bytes=64) for h in range(2)]
         negmax = [sb.tile([P, 1], F32, name="negmax%d" % r) for r in range(PACK)]
         rowsum = [sb.tile([P, 2], F32, name="rowsum%d" % h) for h in range(2)]
         rowinv = [sb.tile([P, 2], F32, name="rowinv%d" % h) for h in range(2)]
@@ -187,36 +202,49 @@ def tile_attend_bmassmerge_pl_kernel(tc, query, keys, mass, target, qs, qrows, o
                 r = 2 * h + e
                 nc.vector.tensor_scalar(pn[:, r, :], p_t[r][:], rowinv[h][:, e : e + 1], qs_t[:, r : r + 1],
                                         ALU.mult, ALU.mult)
-        ds_bf = sb.tile([P, I, PACK], BF16, name="ds_bf", align_bytes=64)
-        nc.vector.tensor_tensor(
-            ds_bf[:].rearrange("p (c i) r -> p c r i", i=RUN),
-            pn[:].rearrange("p r (c i) -> p c r i", i=RUN),
-            tq[:].rearrange("p r (c i) -> p c r i", i=RUN),
-            ALU.subtract,
-        )
-        r_quant = [quantise(qrows_bf[:, 0, :, :].rearrange("p s j -> p (s j)"), P, "qrows0")]
-        ds_codes, ds_scales = quantise(ds_bf[:].rearrange("p i r -> p (i r)"), I, "ds")
+        ds_bf = [sb.tile([P, P, PACK], BF16, name="ds_bf%d" % h, align_bytes=64) for h in range(2)]
+        slot_half = [slice(P * h, P * (h + 1)) for h in range(2)]
+        for h in range(2):
+            nc.vector.tensor_tensor(
+                ds_bf[h][:].rearrange("p (c i) r -> p c r i", i=RUN),
+                pn[:, :, slot_half[h]].rearrange("p r (c i) -> p c r i", i=RUN),
+                tq[:, :, slot_half[h]].rearrange("p r (c i) -> p c r i", i=RUN),
+                ALU.subtract,
+            )
+        ds_codes = sb.tile([P, I], U32, name="ds_codes", align_bytes=64)
+        ds_scales = sb.tile([P, I], U8, name="ds_scales", align_bytes=64)
+        for h in range(2):
+            nc.vector.quantize_mx(out=ds_codes[:, slot_half[h]].bitcast(FP8X4), scales=ds_scales[:, slot_half[h]],
+                                  in_=ds_bf[h][:].rearrange("p i r -> p (i r)"))
 
-        gk = []
-        for j in range(PACK):
-            if j > 0:
-                r_quant.append(quantise(qrows_bf[:, j, :, :].rearrange("p s j -> p (s j)"), P, "qrows%d" % j))
-            acc = bank((6 + j) % 8, [P, I], "gk_acc%d" % j)
+        gk = [sb.tile([P, I], F32, name="gk%d" % j) for j in range(PACK)]
+
+        def gradient(j, slots, number):
+            cols = slice(P * (j % 2), P * (j % 2 + 1))
+            acc = bank(number, [P, slots.stop - slots.start], "gk_acc%d_%d" % (j, slots.start))
             nc.tensor.matmul_mx(
                 out=acc[:],
-                lhsT=r_quant[j][0][:].bitcast(FP8X4), lhsT_scale=r_quant[j][1][:],
-                rhs=ds_codes[:].bitcast(FP8X4), rhs_scale=ds_scales[:],
+                lhsT=r_quant[j // 2][0][:, cols].bitcast(FP8X4), lhsT_scale=r_quant[j // 2][1][:, cols],
+                rhs=ds_codes[:, slots].bitcast(FP8X4), rhs_scale=ds_scales[:, slots],
                 start=True, stop=True,
             )
-            gk.append(sb.tile([P, I], F32, name="gk%d" % j))
-            nc.scalar.copy(gk[j][:], acc[:])
+            nc.scalar.copy(gk[j][:, slots], acc[:])
+
+        all_slots = slice(0, I)
+        for h in range(2):
+            gradient(0, slot_half[h], 6 + h)
+        gradient(1, all_slots, 0)
+        r_quant.append(quantise_qrows(1, "s1"))
+        gradient(2, all_slots, 1)
+        gradient(3, all_slots, 0)
 
         out_v = out_0.rearrange("(p j) t -> p j t", j=PACK)
         y = sb.tile([P, PACK, T], F32, name="y")
         y_bf = [sb.tile([P, CW, PACK], BF16, name="y_bf%d" % c, align_bytes=64) for c in range(CHUNKS)]
 
-        def scatter(n, j):
-            nc.vector.tensor_tensor(win[n][j % 2][:].indirect(list_t[n][:]), gk[j][:], share[:, n, :], ALU.mult)
+        def scatter(n, j, slots=all_slots):
+            offsets = list_t[n][:, slots.start // 16 : slots.stop // 16]
+            nc.vector.tensor_tensor(win[n][j % 2][:].indirect(offsets), gk[j][:, slots], share[:, n, slots], ALU.mult)
 
         def weave(first, last, c, on_scalar):
             dst = y_bf[c][:, :, first:last].rearrange("p (c i) j -> p c j i", i=RUN)
@@ -242,10 +270,12 @@ def tile_attend_bmassmerge_pl_kernel(tc, query, keys, mass, target, qs, qrows, o
         def finish(j, back):
             for g in range(2):
                 nc.scalar.copy(y[:, j, halves[g]], back[g])
-            nc.scalar.dma_start(out_v[:, j, :], y[:, j, :])
+            nc.sync.dma_start(out_v[:, j, :], y[:, j, :])
 
         for n in range(2):
-            scatter(n, 0)
+            scatter(n, 0, slot_half[0])
+        for n in range(2):
+            scatter(n, 0, slot_half[1])
             turn_in(yt_ps[0], win[n][0], False, n == 1)
         finish(0, turn_back(0, 0))
         for n in range(2):
@@ -256,33 +286,28 @@ def tile_attend_bmassmerge_pl_kernel(tc, query, keys, mass, target, qs, qrows, o
         turn_in(yt_ps[2], win[0][0], False, True)
         back = turn_back(2, 0)
         finish(1, back1)
-        for c in range(CHUNKS):
-            weave(0, 1 if c < 2 else 2, c, True)
-        scatter(1, 2)
+        for c in (2, 3):
+            weave(0, 2, c, True)
         scatter(0, 3)
-        scatter(1, 3)
+        scatter(1, 2)
         nc.vector.tensor_tensor(y[:, 3, :], old_t[3][:], win[0][1][:], ALU.add)
-        for g in range(2):
-            nc.vector.tensor_tensor(y[:, 2, halves[g]], back[g], win[1][0][:, halves[g]], ALU.add)
-        nc.sync.dma_start(out_v[:, 2, :], y[:, 2, :])
+        scatter(1, 3)
 
         y_codes = sb.tile([P, T], U32, name="y_codes", align_bytes=64)
         y_scales = sb.tile([P, T], U8, name="y_scales", align_bytes=64)
         words_v = out_1[0].rearrange("l c r -> l (c r)").bitcast(I32)
-        for c in range(CHUNKS):
-            cols = slice(CW * c, CW * (c + 1))
-            nc.vector.tensor_tensor(y[:, 3, cols], y[:, 3, cols], win[1][1][:, cols], ALU.add)
-            if c < 2:
-                weave(1, PACK, c, True)
-            if c % 2 == 1:
-                nc.sync.dma_start(out_v[:, 3, halves[c // 2]], y[:, 3, halves[c // 2]])
+        for g in range(2):
+            nc.vector.tensor_tensor(y[:, 2, halves[g]], back[g], win[1][0][:, halves[g]], ALU.add)
+            nc.vector.tensor_tensor(y[:, 3, halves[g]], y[:, 3, halves[g]], win[1][1][:, halves[g]], ALU.add)
+            nc.sync.dma_start(out_v[:, 2:4, halves[g]], y[:, 2:4, halves[g]])
+        for c in (0, 1):
+            weave(0, PACK, c, True)
         for c in (2, 3):
             weave(2, PACK, c, False)
-        for c in range(CHUNKS):
+        for c in (2, 3, 0, 1):
             cols = slice(CW * c, CW * (c + 1))
             nc.vector.quantize_mx(out=y_codes[:, cols].bitcast(FP8X4), scales=y_scales[:, cols],
                                   in_=y_bf[c][:].rearrange("p t j -> p (t j)"))
-            if c % 2 == 1:
-                nc.sync.dma_start(words_v[:, halves[c // 2]], y_codes[:, halves[c // 2]].bitcast(I32))
+            nc.sync.dma_start(words_v[:, cols], y_codes[:, cols].bitcast(I32))
         for g in range(4):
             (nc.scalar if g < 2 else nc.sync).dma_start(out_2[0, 4 * g : 4 * g + 4, :].bitcast(I32), y_scales[32 * g : 32 * g + 4, :].bitcast(I32))

from contextlib import ExitStack

import concourse.mybir as mybir
from concourse.masks import make_identity

D, T, I, Q = 512, 1024, 256, 512
FLOPS = 2 * D * Q * I * 2

F32 = mybir.dt.float32
BF16 = mybir.dt.bfloat16
I32 = mybir.dt.int32
U32 = mybir.dt.uint32
U16 = mybir.dt.uint16
U8 = mybir.dt.uint8
FP8X4 = mybir.dt.float8_e4m3fn_x4
ALU = mybir.AluOpType
ACT = mybir.ActivationFunctionType
AX = mybir.AxisListType

P = 128
PACK = 4
RUN = 4
CHUNKS = 4
CW = T // CHUNKS


def tile_attend_bmassmerge_pl_kernel(tc, query, keys, mass, target, qs, qrows, old, offs, offs2, out_0, out_1, out_2):
    nc = tc.nc
    with ExitStack() as ctx:
        lists = ctx.enter_context(tc.tile_pool(name="lists", bufs=1))
        sb = ctx.enter_context(tc.tile_pool(name="sb", bufs=1))
        ps = ctx.enter_context(tc.psum_pool(name="ps", bufs=1))

        def bank(number, shape, name):
            return ps.tile(shape, F32, name=name, tag="bank%d" % number)

        ident = sb.tile([P, P], F32, name="ident")
        make_identity(nc, ident[:])

        def turn(dst, src, start=True, stop=True):
            nc.tensor.matmul(dst, src, ident[:], start=start, stop=stop, is_transpose=True)

        mass_t = sb.tile([P, T], F32, name="mass_t")
        nc.sync.dma_start(mass_t[:], mass)
        list_t = [lists.tile([P, I // 16], U16, name="list%d" % n) for n in range(2)]
        nc.sync.dma_start(list_t[0][:], offs)
        nc.sync.dma_start(list_t[1][:], offs2)

        keys_v = keys.rearrange("(p j) t -> p j t", j=PACK)
        key_t = [sb.tile([P, T], F32, name="key%d" % j) for j in range(PACK)]
        for j in range(PACK):
            nc.sync.dma_start(key_t[j][:], keys_v[:, j, :])

        def load_halves(src, halves):
            view = src.rearrange("(p j) c -> p j c", j=PACK)
            for h in range(2):
                nc.sync.dma_start(halves[h][:], view[:, :, 256 * h : 256 * (h + 1)])
            return halves

        query_h = load_halves(query, [sb.tile([P, PACK, 256], F32, name="query_raw%d" % h) for h in range(2)])
        qrows_raw = sb.tile([P, PACK, D], F32, name="qrows_raw")
        nc.sync.dma_start(qrows_raw[:], qrows.rearrange("(p j) c -> p j c", j=PACK))
        qs_t = sb.tile([P, PACK], F32, name="qs_t")
        nc.sync.dma_start(qs_t[:], qs.rearrange("(s r) o -> s (r o)", r=PACK))
        target_t = sb.tile([P, PACK, I], F32, name="target_t")
        nc.sync.dma_start(target_t[:], target.rearrange("(s r) i -> s r i", r=PACK))
        old_v = old.rearrange("(p j) t -> p j t", j=PACK)
        old_t = [sb.tile([P, T], F32, name="old%d" % j) for j in range(PACK)]
        for j in range(PACK):
            nc.sync.dma_start(old_t[j][:], old_v[:, j, :])

        win = [[sb.tile([P, T], F32, name="win%d_%d" % (n, b)) for b in range(2)] for n in range(2)]
        for b in range(2):
            for n in range(2):
                (nc.gpsimd if n + b == 2 else nc.vector).memset(win[n][b][:], 0.0)

        m12 = sb.tile([P, 2, I], F32, name="m12")
        for n in range(2):
            nc.vector.tensor_copy(m12[:, n, :], mass_t[:].indirect(list_t[n][:]))
        msum_ps = bank(1, [P, 2, P], "msum_ps")
        for h in range(2):
            for n in range(2):
                turn(msum_ps[:, h, :], m12[:, n, P * h : P * (h + 1)], start=(n == 0), stop=(n == 1))
        m_ps = bank(0, [P, 2, 2, P], "m_ps")
        for n in range(2):
            for h in range(2):
                turn(m_ps[:, n, h, :], m12[:, n, P * h : P * (h + 1)])
        lncol = sb.tile([P, 2], F32, name="lncol")
        nc.scalar.activation(lncol[:], msum_ps[:, :, 0], ACT.Ln)
        rcol = sb.tile([P, 2], F32, name="rcol")
        nc.vector.reciprocal(rcol[:], msum_ps[:, :, 0])
        sharecol = sb.tile([P, 2, 2], F32, name="sharecol")
        for h in range(2):
            nc.scalar.activation(sharecol[:, :, h], m_ps[:, :, h, 0], ACT.Copy, scale=rcol[:, h : h + 1])
        ln_ps = bank(3, [P, 2, P], "ln_ps")
        for h in range(2):
            turn(ln_ps[:, h, :], lncol[:, h : h + 1].to_broadcast([P, P]))
        share_ps = bank(2, [P, 2, 2, P], "share_ps")
        for n in range(2):
            for h in range(2):
                turn(share_ps[:, n, h, :], sharecol[:, n, h : h + 1].to_broadcast([P, P]))
        lnm = sb.tile([P, I], F32, name="lnm")
        nc.scalar.copy(lnm[:], ln_ps[:].rearrange("p h i -> p (h i)"))
        share = sb.tile([P, 2, I], F32, name="share")
        nc.scalar.copy(share[:], share_ps[:].rearrange("p n h i -> p n (h i)"))

        def deal(halves, name, copies):
            dealt = sb.tile([P, PACK, P, PACK], BF16, name=name + "_bf", align_bytes=64)
            for h in range(2):
                copies[h](
                    dealt[:, :, 64 * h : 64 * (h + 1), :].rearrange("p r s j -> p s j r"),
                    halves[h][:].rearrange("p j (s r) -> p s j r", r=PACK),
                )
            return dealt

        def quantise(src_flat, width, name):
            codes = sb.tile([P, width], U32, name=name + "_codes", align_bytes=64)
            scales = sb.tile([P, width], U8, name=name + "_scales", align_bytes=64)
            nc.vector.quantize_mx(out=codes[:].bitcast(FP8X4), scales=scales[:], in_=src_flat)
            return codes, scales


        wk = [[sb.tile([P, I], F32, name="wk%d_%d" % (n, j)) for j in range(PACK)] for n in range(2)]
        km_back = [bank(h, [P, 2, P], "km_back%d" % h) for h in range(2)]
        for u in range(2):
            km_ps = [bank(4 + 2 * u + h, [P, 2, P], "km_ps%d_%d" % (u, h)) for h in range(2)]
            for e in range(2):
                j = 2 * u + e
                for n in range(2):
                    last = j == PACK - 1 and n == 1
                    if not last:
                        nc.vector.tensor_tensor(wk[n][j][:], key_t[j][:].indirect(list_t[n][:]), m12[:, n, :], ALU.mult)
                    for h in range(2):
                        if last:
                            nc.vector.tensor_tensor(wk[n][j][:, P * h : P * (h + 1)],
                                                    key_t[j][:].indirect(list_t[n][:, 8 * h : 8 * (h + 1)]),
                                                    m12[:, n, P * h : P * (h + 1)], ALU.mult)
                        turn(km_ps[h][:, e, :], wk[n][j][:, P * h : P * (h + 1)], start=(n == 0), stop=(n == 1))
            for h in range(2):
                tag = "qrows_then_tq" if u + h == 2 else "pairs%d_%d" % (u, h)
                pairs = sb.tile([P, P, 2], BF16, name="pairs%d_%d" % (u, h), tag=tag, align_bytes=64)
                nc.scalar.activation(pairs[:], km_ps[h][:].rearrange("i e p -> i p e"), ACT.Copy, scale=rcol[:, h : h + 1])
                turn(km_back[h][:, u, :], pairs[:].rearrange("i p e -> i (p e)").bitcast(F32))
        query_bf = deal(query_h, "query", [nc.scalar.copy, nc.vector.tensor_copy])
        q_codes, q_scales = quantise(query_bf[:].rearrange("p r s j -> p (r s j)"), Q, "query")
        km_bf = sb.tile([P, I * PACK], BF16, name="km_bf", align_bytes=64)
        km_words = km_bf[:].bitcast(F32).rearrange("p (h i u) -> p h i u", h=2, u=2)
        for h in range(2):
            nc.vector.tensor_copy(km_words[:, h, :, :], km_back[h][:].rearrange("p u i -> p i u"))
        km_codes, km_scales = quantise(km_bf[:], I, "km")

        def quantise_qrows(u, tag):
            dealt = sb.tile([P, 2, P, PACK], BF16, name="qrows_bf%d" % u, tag=tag, align_bytes=64)
            nc.scalar.copy(dealt[:].rearrange("p e m j -> p m j e"),
                           qrows_raw[:].rearrange("p j (m t) -> p m j t", t=PACK)[:, :, :, 2 * u : 2 * u + 2])
            return quantise(dealt[:].rearrange("p e m j -> p (e m j)"), 2 * P, "qrows%d" % u)

        r_quant = [quantise_qrows(0, "qrows_then_tq")]
        tq = sb.tile([P, PACK, I], F32, name="tq", tag="qrows_then_tq", align_bytes=64)
        for r in range(PACK):
            nc.gpsimd.tensor_scalar(tq[:, r, :], target_t[:, r, :], qs_t[:, r : r + 1], 0.0, ALU.mult, ALU.add)

        score = [bank(h, [P, 2, I], "score%d" % h) for h in range(2)]
        for r in range(PACK):
            cols = slice(P * r, P * (r + 1))
            nc.tensor.matmul_mx(
                out=score[r // 2][:, r % 2, :],
                lhsT=q_codes[:, cols].bitcast(FP8X4), lhsT_scale=q_scales[:, cols],
                rhs=km_codes[:].bitcast(FP8X4), rhs_scale=km_scales[:],
                start=True, stop=True,
            )

        BLOCKS = T // P

        def open_sum(j, first_bank):
            banks = [bank(first_bank + g, [P, 4, P], "yt_ps%d_%d" % (j, g)) for g in range(2)]
            turn_in(banks, old_t[j], True, False)
            return banks

        def turn_in(banks, src, start, stop):
            for b in range(BLOCKS):
                turn(banks[b // 4][:, b % 4, :], src[:, P * b : P * (b + 1)],
                     start=(start and b % 4 == 0), stop=(stop and b % 4 == 3))

        yt_ps = [open_sum(0, 2), open_sum(1, 4)]

        s_t = [sb.tile([P, 2, I], F32, name="s%d" % h, tag="s%d" % h, align_bytes=64) for h in range(2)]
        negmax = [sb.tile([P, 1], F32, name="negmax%d" % r) for r in range(PACK)]
        rowsum = [sb.tile([P, 2], F32, name="rowsum%d" % h) for h in range(2)]
        rowinv = [sb.tile([P, 2], F32, name="rowinv%d" % h) for h in range(2)]
        p_t = [sb.tile([P, I], F32, name="p%d" % r) for r in range(PACK)]
        pn = sb.tile([P, PACK, I], F32, name="pn")
        for h in range(2):
            nc.vector.tensor_tensor(s_t[h][:], score[h][:], lnm[:].unsqueeze(1).to_broadcast([P, 2, I]), ALU.add)
        for r in range(PACK):
            h, e = divmod(r, 2)
            nc.vector.tensor_reduce(negmax[r][:], s_t[h][:, e, :], AX.X, ALU.max, negate=True)
            nc.scalar.activation(p_t[r][:], s_t[h][:, e, :], ACT.Exp, bias=negmax[r][:], accum_out=rowsum[h][:, e : e + 1])
        for h in range(2):
            nc.vector.reciprocal(rowinv[h][:], rowsum[h][:])
            for e in range(2):
                r = 2 * h + e
                nc.vector.tensor_scalar(pn[:, r, :], p_t[r][:], rowinv[h][:, e : e + 1], qs_t[:, r : r + 1],
                                        ALU.mult, ALU.mult)
        ds_bf = [sb.tile([P, P, PACK], BF16, name="ds_bf%d" % h, align_bytes=64) for h in range(2)]
        slot_half = [slice(P * h, P * (h + 1)) for h in range(2)]
        for h in range(2):
            nc.vector.tensor_tensor(
                ds_bf[h][:].rearrange("p (c i) r -> p c r i", i=RUN),
                pn[:, :, slot_half[h]].rearrange("p r (c i) -> p c r i", i=RUN),
                tq[:, :, slot_half[h]].rearrange("p r (c i) -> p c r i", i=RUN),
                ALU.subtract,
            )
        ds_codes = sb.tile([P, I], U32, name="ds_codes", align_bytes=64)
        ds_scales = sb.tile([P, I], U8, name="ds_scales", align_bytes=64)
        for h in range(2):
            nc.vector.quantize_mx(out=ds_codes[:, slot_half[h]].bitcast(FP8X4), scales=ds_scales[:, slot_half[h]],
                                  in_=ds_bf[h][:].rearrange("p i r -> p (i r)"))

        gk = [sb.tile([P, I], F32, name="gk%d" % j) for j in range(PACK)]

        def gradient(j, slots, number):
            cols = slice(P * (j % 2), P * (j % 2 + 1))
            acc = bank(number, [P, slots.stop - slots.start], "gk_acc%d_%d" % (j, slots.start))
            nc.tensor.matmul_mx(
                out=acc[:],
                lhsT=r_quant[j // 2][0][:, cols].bitcast(FP8X4), lhsT_scale=r_quant[j // 2][1][:, cols],
                rhs=ds_codes[:, slots].bitcast(FP8X4), rhs_scale=ds_scales[:, slots],
                start=True, stop=True,
            )
            nc.scalar.copy(gk[j][:, slots], acc[:])

        all_slots = slice(0, I)
        for h in range(2):
            gradient(0, slot_half[h], 6 + h)
        gradient(1, all_slots, 0)
        r_quant.append(quantise_qrows(1, "s1"))
        gradient(2, all_slots, 1)
        gradient(3, all_slots, 0)

        out_v = out_0.rearrange("(p j) t -> p j t", j=PACK)
        y = sb.tile([P, PACK, T], F32, name="y")
        y_bf = [sb.tile([P, CW, PACK], BF16, name="y_bf%d" % c, align_bytes=64) for c in range(CHUNKS)]

        def scatter(n, j, slots=all_slots):
            offsets = list_t[n][:, slots.start // 16 : slots.stop // 16]
            nc.vector.tensor_tensor(win[n][j % 2][:].indirect(offsets), gk[j][:, slots], share[:, n, slots], ALU.mult)

        def weave(first, last, c, on_scalar):
            dst = y_bf[c][:, :, first:last].rearrange("p (c i) j -> p c j i", i=RUN)
            src = y[:, first:last, CW * c : CW * (c + 1)].rearrange("p j (c i) -> p c j i", i=RUN)
            if on_scalar:
                nc.scalar.copy(dst, src)
            else:
                nc.vector.tensor_copy(dst, src)

        def turn_back(j, first_bank):
            yt = [sb.tile([P, 4, P], F32, name="yt%d_%d" % (j, g)) for g in range(2)]
            for g in range(2):
                nc.scalar.copy(yt[g][:], yt_ps[j][g][:])
            back = []
            for g in range(2):
                back.append(bank(first_bank + g, [P, 4, P], "back%d_%d" % (j, g)))
                for b in range(4):
                    turn(back[g][:, b, :], yt[g][:, b, :])
            return [tile[:].rearrange("p b t -> p (b t)") for tile in back]

        halves = [slice(512 * g, 512 * (g + 1)) for g in range(2)]
        yt_ps.append(open_sum(2, 6))
        def finish(j, back):
            for g in range(2):
                nc.scalar.copy(y[:, j, halves[g]], back[g])
            nc.sync.dma_start(out_v[:, j, :], y[:, j, :])

        for n in range(2):
            scatter(n, 0, slot_half[0])
        for n in range(2):
            scatter(n, 0, slot_half[1])
            turn_in(yt_ps[0], win[n][0], False, n == 1)
        finish(0, turn_back(0, 0))
        for n in range(2):
            scatter(n, 1)
            turn_in(yt_ps[1], win[n][1], False, n == 1)
        back1 = turn_back(1, 2)
        scatter(0, 2)
        turn_in(yt_ps[2], win[0][0], False, True)
        back = turn_back(2, 0)
        finish(1, back1)
        for c in (2, 3):
            weave(0, 2, c, True)
        scatter(0, 3)
        scatter(1, 2)
        nc.vector.tensor_tensor(y[:, 3, :], old_t[3][:], win[0][1][:], ALU.add)
        scatter(1, 3)

        y_codes = sb.tile([P, T], U32, name="y_codes", align_bytes=64)
        y_scales = sb.tile([P, T], U8, name="y_scales", align_bytes=64)
        words_v = out_1[0].rearrange("l c r -> l (c r)").bitcast(I32)
        for g in range(2):
            nc.vector.tensor_tensor(y[:, 2, halves[g]], back[g], win[1][0][:, halves[g]], ALU.add)
            nc.vector.tensor_tensor(y[:, 3, halves[g]], y[:, 3, halves[g]], win[1][1][:, halves[g]], ALU.add)
            nc.sync.dma_start(out_v[:, 2:4, halves[g]], y[:, 2:4, halves[g]])
        for c in (0, 1):
            weave(0, PACK, c, True)
        for c in (2, 3):
            weave(2, PACK, c, False)
        for c in (2, 3, 0, 1):
            cols = slice(CW * c, CW * (c + 1))
            nc.vector.quantize_mx(out=y_codes[:, cols].bitcast(FP8X4), scales=y_scales[:, cols],
                                  in_=y_bf[c][:].rearrange("p t j -> p (t j)"))
            nc.sync.dma_start(words_v[:, cols], y_codes[:, cols].bitcast(I32))
        for g in range(4):
            (nc.scalar if g < 2 else nc.sync).dma_start(out_2[0, 4 * g : 4 * g + 4, :].bitcast(I32), y_scales[32 * g : 32 * g + 4, :].bitcast(I32))
